import numpy as np
import ml_dtypes


def mxq(x, axis, fmt="e4m3"):
    dtype, down = {"e4m3": (ml_dtypes.float8_e4m3fn, 7), "e5m2": (ml_dtypes.float8_e5m2, 14)}[fmt]
    v = np.moveaxis(np.asarray(x, np.float32).astype(ml_dtypes.bfloat16).astype(np.float64), axis, -1)
    blocks = v.reshape(v.shape[:-1] + (-1, 32))
    amax = np.abs(blocks).max(-1, keepdims=True)
    byte = np.maximum(np.where(amax > 0, np.frexp(amax)[1] - 1 + 127, 0) - down, 1)
    scale = np.exp2(byte - 127.0)
    codes = (blocks / scale).astype(np.float32).astype(dtype).astype(np.float64)
    return np.moveaxis((codes * scale).reshape(v.shape), -1, axis)


WIDE = False


def mx_kscale(k):
    if not WIDE:
        return np.ones(k)
    levels = np.array([10, -10, 5, -5, 0])
    if k % 512:
        return np.exp2(np.random.permutation(np.resize(levels, k // 32))).repeat(32)
    a = np.empty((k // 512, 16))
    for p in range(k // 512):
        a[p, :8] = np.random.permutation(np.resize(levels, 8))
        for g in range(8):
            far = levels[np.abs(levels - a[p, g]) >= 10]
            a[p, g + 8] = far[np.random.randint(len(far))]
    return np.exp2(a.ravel()).repeat(32)


BF16 = ml_dtypes.bfloat16


def bf(x):
    return np.asarray(x, np.float32).astype(BF16)


def f64(x):
    return np.asarray(x).astype(np.float64)


E2M1 = np.array([0.0, 0.5, 1.0, 1.5, 2.0, 3.0, 4.0, 6.0, -0.0, -0.5, -1.0, -1.5, -2.0, -3.0, -4.0, -6.0])


def pack_weight(w, fmt):
    k, n = w.shape
    w = f64(bf(w)).reshape(k // 32, 32, n)
    amax = np.abs(w).max(1)
    if fmt == "e4m3":
        byte = np.frexp(amax)[1] - 1 + 127 - 7
    else:
        mant, ex = np.frexp(amax / 6.0)
        byte = np.where(mant > 0.5, ex, ex - 1) + 127
    byte = np.clip(np.where(amax > 0, byte, 1), 1, 254)
    scaled = (w * np.exp2(127.0 - byte)[:, None, :]).reshape(k, n).astype(np.float32)
    by_word = np.ascontiguousarray(scaled.reshape(k // 512, 128, 4, n).transpose(0, 1, 3, 2))
    if fmt == "e4m3":
        words = by_word.astype(ml_dtypes.float8_e4m3fn).view(np.uint8)
    else:
        c = by_word.astype(ml_dtypes.float4_e2m1fn).view(np.uint8) & 0xF
        words = c[..., 0::2] | (c[..., 1::2] << 4)
    return np.ascontiguousarray(words), np.ascontiguousarray(byte.astype(np.uint8).reshape(k // 512, 16, n))


def unpack_weight(words, scales, fmt):
    g, p, n, _ = words.shape
    if fmt == "e4m3":
        vals = np.ascontiguousarray(words).view(ml_dtypes.float8_e4m3fn).astype(np.float64)
    else:
        nib = np.empty((g, p, n, 4), np.uint8)
        nib[..., 0::2] = words & 0xF
        nib[..., 1::2] = words >> 4
        vals = E2M1[nib]
    vals = vals * np.repeat(np.exp2(scales.astype(np.float64) - 127.0), 8, axis=1)[..., None]
    return vals.transpose(0, 1, 3, 2).reshape(g * 512, n)
def pack4(w):
    words, scales = pack_weight(w, "e2m1")
    return words.reshape(words.shape[0], 128, -1), scales


def unpack4(words, scales):
    return unpack_weight(words.reshape(words.shape[0], 128, -1, 2), scales, "e2m1")


E, R, K, M, N = 512, 4, 512, 1024, 1536
P = E * R


def draw0():
    s = mx_kscale(K)
    t = mx_kscale(P)
    tm = t.reshape(E, R)[:, 0]
    right = np.random.standard_normal((P, N)) / np.sqrt(P) / t[:, None]
    right_words, right_scales = pack4(right)
    return {"z": bf(np.random.standard_normal((P, K)) * s),
            "c": bf(np.random.standard_normal((K, M)) / np.sqrt(K) / s[:, None]),
            "fitness": bf(np.random.standard_normal(E) * tm),
            "right_words": right_words,
            "right_scales": right_scales,
            "eta": bf(1 + 0.1 * np.random.standard_normal(M)),
            "theta": bf(0.5 * np.random.standard_normal((M, N)))}


def core(z, c, fitness, right_words, right_scales, eta, theta):
    left = mxq(f64(z), 1, "e4m3") @ mxq(f64(c), 0, "e4m3")
    h = (left.reshape(E, R, M) * f64(fitness)[:, None, None]).reshape(P, M)
    b = unpack4(right_words, right_scales)
    g = mxq(h, 0, "e4m3").T @ b
    return f64(theta) + f64(eta)[:, None] * g


def e4m3fn_bytes(y):
    return np.clip(np.asarray(y, np.float64), -448.0, 448.0).astype(np.float32).astype(ml_dtypes.float8_e4m3fn).view(np.uint8)


def e4m3fn_values(b):
    return np.asarray(b, np.uint8).view(ml_dtypes.float8_e4m3fn).astype(np.float64)


def setup_inputs():
    d = draw0()
    x0 = np.asarray(d['z']).astype(np.float64)
    s = (np.max(np.abs(x0), axis=(0,), keepdims=True) / 448.0).astype(np.float32)
    out = {}
    for k, v in d.items():
        if k == 'z':
            out['z_bytes'] = e4m3fn_bytes(x0 / s.astype(np.float64))
            out['z_scale'] = s
        else:
            out[k] = v
    return out


def reference(z_bytes, z_scale, c, fitness, right_words, right_scales, eta, theta):
    return core(e4m3fn_values(z_bytes) * z_scale.astype(np.float64), c, fitness, right_words, right_scales, eta, theta)

from contextlib import ExitStack

import concourse.mybir as mybir
from concourse.masks import make_identity

E, R, K, M, N = 512, 4, 512, 1024, 1536
POP = E * R
FLOPS = 2 * POP * K * M + 2 * POP * M * N

F32 = mybir.dt.float32
BF16 = mybir.dt.bfloat16
U32 = mybir.dt.uint32
I32 = mybir.dt.int32
U8 = mybir.dt.uint8
FP8 = mybir.dt.float8_e4m3fn
FP8X4 = mybir.dt.float8_e4m3fn_x4
FP4X4 = mybir.dt.float4_e2m1fn_x4
MULT = mybir.AluOpType.mult
ADD = mybir.AluOpType.add
COPY = mybir.ActivationFunctionType.Copy

P = 128
G = POP // 512
MT = M // P
NB = 3


def tile_low_rank_es_update_s13_kernel(
    tc, z_bytes, z_scale, c, fitness, right_words, right_scales, eta, theta, out
):
    nc = tc.nc
    with ExitStack() as ctx:
        keep = ctx.enter_context(tc.tile_pool(name="keep", bufs=1))
        stage = ctx.enter_context(tc.tile_pool(name="stage", bufs=6))
        ht = ctx.enter_context(tc.psum_pool(name="ht", bufs=3))
        acc = ctx.enter_context(tc.psum_pool(name="acc", bufs=5))
        ctx.enter_context(tc.manual_schedule())

        def sb(shape, dtype, name):
            return keep.tile(shape, dtype, name=name, align_bytes=64)

        ident = sb([P, P], F32, "ident")
        ident_bf = sb([P, P], BF16, "ident_bf")
        s_bc = sb([P, K], F32, "s_bc")
        fe = sb([P, P], BF16, "fe")
        fit_eta = sb([P, 16], F32, "fit_eta")
        z_raw = [sb([P, 4 * K], U8, "z_raw%d" % g) for g in range(G)]
        z_bf = [sb([P, 4, K], BF16, "z_bf%d" % g) for g in range(G)]
        z_grp = [sb([P, 512, 4], BF16, "z_grp%d" % g) for g in range(G)]
        z_code = [sb([P, 512], U32, "z_code%d" % g) for g in range(G)]
        z_sc = [sb([P, 512], U8, "z_sc%d" % g) for g in range(G)]
        c_raw = [sb([P, 4, 512], BF16, "c_raw%d" % i) for i in range(2)]
        c_grp = [sb([P, 256, 4], BF16, "c_grp%d" % j) for j in range(MT // 2)]
        c_code = [sb([P, 256], U32, "c_code%d" % j) for j in range(MT // 2)]
        c_sc = [sb([P, 256], U8, "c_sc%d" % j) for j in range(MT // 2)]
        h_bf = [sb([P, G, 2, 512], BF16, "h_bf%d" % j) for j in range(MT // 2)]
        h_code = [sb([P, G, 2, P], U32, "h_code%d" % j) for j in range(MT // 2)]
        h_sc = [sb([P, G, 2, P], U8, "h_sc%d" % j) for j in range(MT // 2)]
        w = [sb([P, 2 * N], U8, "w%d" % g) for g in range(G)]
        w_sc = sb([P, G, N], U8, "w_sc")
        th = [sb([P, N], BF16, "th%d" % m) for m in range(MT)]

        z_view = z_bytes.rearrange("(g m t) k -> g m (t k)", m=P, t=4)
        c_view = c.rearrange("(p j) w -> p j w", j=4)
        theta_view = theta.rearrange("(m p) n -> m p n", p=P)
        out_view = out.rearrange("(m p) n -> m p n", p=P)

        nc.vector.memset(fe[:], 0.0)
        nc.vector.memset(w_sc[:].rearrange("p g n -> p (g n)").bitcast(I32), 0)
        make_identity(nc, ident[:])
        make_identity(nc, ident_bf[:])

        nc.scalar.dma_start(out=s_bc[:], in_=z_scale.rearrange("o k -> (o k)").partition_broadcast(P))
        nc.scalar.dma_start(out=fe[0:4, :], in_=fitness.rearrange("(g p) -> g p", p=P))
        nc.scalar.dma_start(out=fe[4:12, :], in_=eta.rearrange("(m p) -> m p", p=P))
        nc.sync.dma_start(out=z_raw[0][:], in_=z_view[0])
        nc.sync.dma_start(out=c_raw[0][:], in_=c_view[:, :, 0:512])
        nc.sync.dma_start(out=z_raw[1][:], in_=z_view[1])
        nc.sync.dma_start(out=z_raw[2][:], in_=z_view[2])
        nc.sync.dma_start(out=c_raw[1][:], in_=c_view[:, :, 512:1024])
        for q in range(4):
            nc.sync.dma_start(
                out=w_sc[32 * q : 32 * q + 4].bitcast(I32),
                in_=right_scales[:, 4 * q : 4 * q + 4, :].rearrange("g q n -> q g n").bitcast(I32),
            )
        nc.sync.dma_start(out=w[0][:], in_=right_words[0])
        nc.sync.dma_start(out=z_raw[3][:], in_=z_view[3])
        for g in range(1, G):
            nc.sync.dma_start(out=w[g][:], in_=right_words[g])
        for m in range(MT):
            nc.sync.dma_start(out=th[m][:], in_=theta_view[m])

        def product(g, t):
            z8 = z_raw[g][:, t * K : (t + 1) * K].bitcast(FP8)
            nc.vector.tensor_tensor(out=z_bf[g][:, t, :], in0=z8, in1=s_bc[:], op=MULT)

        banks = {}
        ON_VECTOR = {(3, 0), (3, 2)}

        def transposes(g, h):
            bank = ht.tile([P, 512], F32, name="bank")
            for t in (0, 1):
                words = z_bf[g][:, 2 * h + t, :].bitcast(F32)
                for u in (0, 1):
                    lo = 256 * u + P * t
                    nc.tensor.transpose(bank[:, lo : lo + P], words[:, u::2], ident[:])
            banks[g, h] = bank

        def copy_z(g, h):
            dst = z_grp[g][:, 256 * h : 256 * h + 256, :].rearrange("p r e -> p (r e)").bitcast(F32)
            nc.scalar.copy(
                out=dst.rearrange("p (r u) -> p r u", u=2), in_=banks[g, h][:].rearrange("p (u r) -> p r u", u=2)
            )

        def quant_z(g):
            nc.vector.quantize_mx(
                out=z_code[g][:].bitcast(FP8X4), scales=z_sc[g][:], in_=z_grp[g][:].rearrange("p r e -> p (r e)")
            )

        def interleave_c(j):
            src = c_raw[j // 2][:, :, 256 * (j % 2) : 256 * (j % 2) + 256]
            nc.gpsimd.tensor_scalar(
                out=c_grp[j][:], in0=src.rearrange("p t w -> p w t"), scalar1=1.0, scalar2=0.0, op0=MULT, op1=ADD
            )

        def quant_c(j):
            nc.vector.quantize_mx(
                out=c_code[j][:].bitcast(FP8X4), scales=c_sc[j][:], in_=c_grp[j][:].rearrange("p w t -> p (w t)")
            )

        def first(g, m):
            j, i = divmod(m, 2)
            cols = slice(P * i, P * i + P)
            bank = ht.tile([P, 512], F32, name="bank")
            for t in range(4):
                rows = slice(P * t, P * t + P)
                nc.tensor.matmul_mx(
                    out=bank[:, rows],
                    lhsT=z_code[g][:, rows].bitcast(FP8X4),
                    lhsT_scale=z_sc[g][:, rows],
                    rhs=c_code[j][:, cols].bitcast(FP8X4),
                    rhs_scale=c_sc[j][:, cols],
                    start=True,
                    stop=True,
                )
            banks[g, m, "h"] = bank

        def copy_h(g, m):
            j, i = divmod(m, 2)
            dst = h_bf[j][:, g, i, :].rearrange("p (m t) -> p m t", t=4)
            src = banks[g, m, "h"][:].rearrange("p (t m) -> p m t", t=4)
            weight = fit_eta[:, g : g + 1]
            if (g, m) in ON_VECTOR:
                nc.vector.tensor_scalar(out=dst, in0=src, scalar1=weight, scalar2=None, op0=MULT)
            else:
                nc.scalar.activation(out=dst, in_=src, func=COPY, scale=weight)

        def quant_h(g, j):
            nc.vector.quantize_mx(
                out=h_code[j][:, g].rearrange("p i w -> p (i w)").bitcast(FP8X4),
                scales=h_sc[j][:, g].rearrange("p i w -> p (i w)"),
                in_=h_bf[j][:, g].rearrange("p i w -> p (i w)"),
            )

        sums = {}

        def second(m, n, g):
            j, i = divmod(m, 2)
            if g == 0:
                sums[m, n] = acc.tile([P, 512], F32, name="sum")
            nc.tensor.matmul_mx(
                out=sums[m, n][:],
                lhsT=h_code[j][:, g, i, :].bitcast(FP8X4),
                lhsT_scale=h_sc[j][:, g, i, :],
                rhs=w[g][:, 1024 * n : 1024 * n + 1024].bitcast(FP4X4),
                rhs_scale=w_sc[:, g, 512 * n : 512 * n + 512],
                start=(g == 0),
                stop=(g == G - 1),
            )

        def finish(m, n):
            cols = slice(512 * n, 512 * n + 512)
            res = stage.tile([P, 512], F32, name="res")
            nc.vector.scalar_tensor_tensor(
                out=res[:],
                in0=sums[m, n][:],
                scalar=fit_eta[:, 4 + m : 5 + m],
                in1=th[m][:, cols],
                op0=MULT,
                op1=ADD,
            )
            nc.sync.dma_start(out=out_view[m][:, cols], in_=res[:])

        steps = []

        def at(slot, step, *args):
            steps.append((slot, len(steps), step, args))

        def turn_fit_eta():
            bank = ht.tile([P, 512], F32, name="bank")
            nc.tensor.matmul(bank[:, 0:16], lhsT=fe[:], rhs=ident_bf[:, 0:16], start=True, stop=True)
            nc.scalar.copy(out=fit_eta[:], in_=bank[:, 0:16])

        EARLY = [(0, 0), (0, 1), (0, 2), (1, 0), (1, 1)]
        at(12, turn_fit_eta)
        for g in range(G):
            for t in range(4):
                at(10 * g + 3 * t, product, g, t)
            for h in (0, 1):
                at(10 * g + 6 * h + 5, transposes, g, h)
                at(10 * g + 6 * h + 6, copy_z, g, h)
            at(10 * g + 15, quant_z, g)
        for j in range(MT // 2):
            at(j - 8, interleave_c, j)
            at(15 + 8 * j - (j == 0), quant_c, j)
        ready = {}
        for m in range(MT):
            for g in range(G):
                slot = max(17 + 7 * g + 5 * m, 15.5 + 10 * g + 0.1 * m)
                at(slot, first, g, m)
                at(slot + 1, copy_h, g, m)
                ready[g, m // 2] = slot + 3
        for g, j in ready:
            at(ready[g, j], quant_h, g, j)
        slot = 0
        for g in range(G):
            slot = max(slot, ready[g, 0]) + 2
            for i, (m, n) in enumerate(EARLY):
                at(slot + i, second, m, n, g)
                if g == G - 1:
                    at(slot + i + 2, finish, m, n)
        slot += len(EARLY)
        for m in range(MT):
            for n in range(NB):
                if (m, n) not in EARLY:
                    slot = max([slot] + [ready[g, m // 2] + 0.1 for g in range(G)])
                    for g in range(G):
                        at(slot, second, m, n, g)
                    at(slot + 2, finish, m, n)
                    slot += 2
        for slot, order, step, args in sorted(steps, key=lambda s: s[:2]):
            step(*args)
